import numpy as np
import ml_dtypes


def mxq(x, axis, fmt="e4m3"):
    dtype, down = {"e4m3": (ml_dtypes.float8_e4m3fn, 7), "e5m2": (ml_dtypes.float8_e5m2, 14)}[fmt]
    v = np.moveaxis(np.asarray(x, np.float32).astype(ml_dtypes.bfloat16).astype(np.float64), axis, -1)
    blocks = v.reshape(v.shape[:-1] + (-1, 32))
    amax = np.abs(blocks).max(-1, keepdims=True)
    byte = np.maximum(np.where(amax > 0, np.frexp(amax)[1] - 1 + 127, 0) - down, 1)
    scale = np.exp2(byte - 127.0)
    codes = (blocks / scale).astype(np.float32).astype(dtype).astype(np.float64)
    return np.moveaxis((codes * scale).reshape(v.shape), -1, axis)


WIDE = False


def mx_kscale(k):
    if not WIDE:
        return np.ones(k)
    levels = np.array([10, -10, 5, -5, 0])
    if k % 512:
        return np.exp2(np.random.permutation(np.resize(levels, k // 32))).repeat(32)
    a = np.empty((k // 512, 16))
    for p in range(k // 512):
        a[p, :8] = np.random.permutation(np.resize(levels, 8))
        for g in range(8):
            far = levels[np.abs(levels - a[p, g]) >= 10]
            a[p, g + 8] = far[np.random.randint(len(far))]
    return np.exp2(a.ravel()).repeat(32)


def f64(x):
    return np.asarray(x).astype(np.float64)


def striped(idx):
    return np.tile(idx.reshape(-1, 16).T, (8, 1)).astype(np.uint16)


def unstriped(offs):
    return offs[:16].T.reshape(-1).astype(np.int64)


def striped8(idx):
    return np.concatenate([x.reshape(-1, 16).T for x in idx]).astype(np.uint16)


def runs(offs, k):
    lists = np.stack([offs[16 * r : 16 * r + 16].T.reshape(-1) for r in range(8)]).astype(np.int64)
    return lists[np.arange(k) % 512 // 64]


def pack_weight(w):
    k, n = w.shape
    w = f64(np.asarray(w, np.float32).astype(ml_dtypes.bfloat16)).reshape(k // 32, 32, n)
    amax = np.abs(w).max(1)
    byte = np.clip(np.where(amax > 0, np.frexp(amax)[1] - 1 + 127 - 7, 1), 1, 254)
    scaled = (w * np.exp2(127.0 - byte)[:, None, :]).reshape(k, n).astype(np.float32)
    words = np.ascontiguousarray(scaled.reshape(k // 512, 128, 4, n).transpose(0, 1, 3, 2)).astype(ml_dtypes.float8_e4m3fn).view(np.uint8)
    return words, np.ascontiguousarray(byte.astype(np.uint8).reshape(k // 512, 16, n))


def unpack_weight(words, scales):
    g, p, n, _ = words.shape
    vals = np.ascontiguousarray(words).view(ml_dtypes.float8_e4m3fn).astype(np.float64) * np.repeat(np.exp2(scales.astype(np.float64) - 127.0), 8, axis=1)[..., None]
    return vals.transpose(0, 1, 3, 2).reshape(g * 512, n)


def sigmoid(v):
    return 1.0 / (1.0 + np.exp(-np.maximum(v, -700.0)))


K, T, S, N, G, H, W = 512, 1024, 256, 512, 2048, 512, 128


def setup_inputs():
    n = np.random.standard_normal
    s = mx_kscale(K)[:, None]
    u = mx_kscale(K)
    packed_xT = pack_weight(n((K, T)) * s)
    packed_dT = pack_weight(n((K, G)) / s)
    packed_w1 = pack_weight(n((H, N)) / np.sqrt(2 * H) / u[:, None])
    packed_w2 = pack_weight(n((K, N)) / np.sqrt(2 * K) / s)
    perm = np.random.permutation(S)
    perm2 = np.random.permutation(S)
    return {
        "x_words": packed_xT[0],
        "x_scales": packed_xT[1],
        "d_words": packed_dT[0],
        "d_scales": packed_dT[1],
        "sl": np.random.uniform(1.0, 2.0, (H, 1)).astype(np.float32),
        "th": (0.5 * n((H, 1))).astype(np.float32),
        "gn": (np.random.uniform(0.5, 1.5, (H, 1)) * u[:, None]).astype(np.float32),
        "w1_words": packed_w1[0],
        "w1_scales": packed_w1[1],
        "w2_words": packed_w2[0],
        "w2_scales": packed_w2[1],
        "offs": striped(np.random.permutation(T)[:S]),
        "k1": striped8(np.random.randint(0, G, (8, H))),
        "hz": striped8(np.random.randint(0, T, (8, S))),
        "k2": striped8(np.random.randint(0, G, (8, H))),
        "hy": striped8(np.random.randint(0, T, (8, S))),
        "k3": striped8(np.random.randint(0, G, (8, H))),
        "n1": striped(np.random.permutation(S)),
        "n2": striped(np.random.permutation(S)),
        "two": striped(np.random.permutation(T)[:S]),
        "n3": striped(perm[:W]),
        "n4": striped(perm[W:]),
        "n5": striped(perm2[:W]),
        "n6": striped(perm2[W:]),
        "n7": striped(np.random.permutation(S)),
    }


def reference(x_words, x_scales, d_words, d_scales, sl, th, gn, w1_words, w1_scales, w2_words, w2_scales, offs, k1, hz, k2, hy, k3, n1, n2, two, n3, n4, n5, n6, n7):
    d_k1 = unpack_weight(d_words, d_scales)[np.arange(K)[:, None], runs(k1, K)]
    xq = unpack_weight(x_words, x_scales)[:, unstriped(offs)]
    d_k2 = unpack_weight(d_words, d_scales)[np.arange(K)[:, None], runs(k2, K)]
    x_hz = unpack_weight(x_words, x_scales)[np.arange(K)[:, None], runs(hz, K)]
    d_k3 = unpack_weight(d_words, d_scales)[np.arange(K)[:, None], runs(k3, K)]
    x_hy = unpack_weight(x_words, x_scales)[np.arange(K)[:, None], runs(hy, K)]
    h = 0.0625 * (d_k1.T @ xq + d_k2.T @ x_hz + d_k3.T @ x_hy)
    ds = np.zeros((H, S))
    ds[:, unstriped(n1)] = h
    sg = sigmoid(f64(sl) * (ds[:, unstriped(n2)] - f64(th)))
    z = f64(gn) * (h * sg)
    x_two = unpack_weight(x_words, x_scales)[:, unstriped(two)]
    h2 = unpack_weight(w1_words, w1_scales).T @ mxq(z, 0, "e4m3") + unpack_weight(w2_words, w2_scales).T @ x_two
    pa = h2[:, unstriped(n3)]
    pb = h2[:, unstriped(n4)]
    rb = np.maximum(pa, pb)
    ua = np.zeros((N, S))
    ua[:, unstriped(n5)] = pb
    ub = ua.copy()
    ub[:, unstriped(n6)] = rb
    return ub - h2[:, unstriped(n7)]

@@ -1,0 +1,312 @@
+from contextlib import ExitStack
+
+import concourse.mybir as mybir
+from concourse.masks import make_identity
+
+FLOPS = 671088640
+
+F32 = mybir.dt.float32
+BF16 = mybir.dt.bfloat16
+I32 = mybir.dt.int32
+U32 = mybir.dt.uint32
+U16 = mybir.dt.uint16
+U8 = mybir.dt.uint8
+FP8X4 = mybir.dt.float8_e4m3fn_x4
+ACT = mybir.ActivationFunctionType
+ALU = mybir.AluOpType
+
+P = 128
+T, G, S, H, N, W = 1024, 2048, 256, 512, 512, 128
+HALF = S // 2
+CHUNK = 256
+DS_COLS = 2 * S
+H2_COLS = S + 16
+
+
+def tile_picked_mthhznterlcpsw_none_p_kernel(
+    tc, x_words, x_scales, d_words, d_scales, sl, th, gn, w1_words, w1_scales, w2_words, w2_scales,
+    offs, k1, hz, k2, hy, k3, n1, n2, two, n3, n4, n5, n6, n7, out,
+):
+    nc = tc.nc
+    with ExitStack() as ctx:
+        lists = ctx.enter_context(tc.tile_pool(name="lists", bufs=1))
+        keep = ctx.enter_context(tc.tile_pool(name="keep", bufs=1))
+        relay = ctx.enter_context(tc.tile_pool(name="relay", bufs=1))
+        psum = ctx.enter_context(tc.psum_pool(name="psum", bufs=1))
+
+        def sb(name, shape, dtype, tag=None):
+            return keep.tile(shape, dtype, name=name, tag=tag or name, align_bytes=64)
+
+        def bank(index, name, shape, dtype=F32):
+            return psum.tile(shape, dtype, name=name, tag="bank%d" % index)
+
+        def load_list(name, src):
+            tile = lists.tile(list(src.shape), U16, name=name)
+            nc.sync.dma_start(tile[:], src)
+            return tile
+
+        def zeroed_plane(name, cols, tag=None):
+            plane = sb(name, [P, cols], U8, tag)
+            nc.vector.memset(plane[:].bitcast(I32), 0)
+            return plane
+
+        def load_words(queue, name, src, tag=None):
+            tile = sb(name, [P, src.shape[2]], U32, tag)
+            queue.dma_start(tile[:].bitcast(I32), src[0].rearrange("p n t -> p (n t)").bitcast(I32))
+            return tile
+
+        def place_rows(queue, plane, picked):
+            for s in range(4):
+                queue.dma_start(plane[:].bitcast(I32)[s:P:32, :], picked[:].bitcast(I32)[8 * s:P:32, :])
+
+        def entries(tile, first, count):
+            return tile[:, first // 16:(first + count) // 16]
+
+        def load_scale_window(name, src):
+            cols = src.shape[2]
+            tile = sb(name, [P, cols], U8)
+            nc.sync.dma_start(
+                tile[:].bitcast(I32), src[0].bitcast(I32).unsqueeze(1).to_broadcast([16, 8, cols // 4])
+            )
+            return tile
+
+        xs_win = load_scale_window("xs_win", x_scales)
+        x_lists = [load_list("offs_sb", offs), load_list("hz_sb", hz), load_list("hy_sb", hy)]
+        ds_win = load_scale_window("ds_win", d_scales)
+        d_lists = [load_list("k1_sb", k1), load_list("k2_sb", k2), load_list("k3_sb", k3)]
+        xw_win = load_words(nc.sync, "xw_win", x_words)
+        dw_win = load_words(nc.sync, "dw_win", d_words)
+        n1_sb = load_list("n1_sb", n1)
+        n2_sb = load_list("n2_sb", n2)
+        two_sb = load_list("two_sb", two)
+        n3_sb = load_list("n3_sb", n3)
+        n4_sb = load_list("n4_sb", n4)
+        n5_sb = load_list("n5_sb", n5)
+        n7_sb = load_list("n7_sb", n7)
+        n6_sb = load_list("n6_sb", n6)
+        plane_a = zeroed_plane("plane_a", 3 * S + 3 * CHUNK)
+        plane_b = zeroed_plane("plane_b", 3 * CHUNK)
+        plane_two = zeroed_plane("plane_two", S)
+
+        ident = sb("ident", [P, P], F32)
+        make_identity(nc, ident[:])
+        ds = [sb("ds%d" % t, [P, DS_COLS], F32) for t in range(4)]
+        h2 = [sb("h2_%d" % m, [P, H2_COLS], F32) for m in range(4)]
+        for t in range(4):
+            nc.gpsimd.memset(ds[t][:, S:], 0.0)
+        for m in range(4):
+            nc.gpsimd.memset(h2[m][:, S:], 0.0)
+        ident_bf = sb("ident_bf", [P, P], BF16)
+        nc.scalar.activation(ident_bf[:], ident[:], ACT.Copy)
+
+        picked_a = relay.tile([P, 3 * S + 3 * CHUNK], U8, name="picked_a", offset=3008)
+        for g in range(3):
+            nc.vector.tensor_copy(picked_a[:, g * S:(g + 1) * S], xs_win[:].indirect(x_lists[g][:]))
+        for g in range(3):
+            nc.vector.tensor_copy(
+                picked_a[:, 3 * S + g * CHUNK:3 * S + (g + 1) * CHUNK],
+                ds_win[:].indirect(entries(d_lists[g], 0, CHUNK)),
+            )
+        place_rows(nc.scalar, plane_a, picked_a)
+
+        rows = relay.tile([P, P], F32, name="rows", offset=3840)
+        nc.gpsimd.memset(rows[:], 0.0)
+        for r, vec in enumerate((sl, th, gn)):
+            nc.sync.dma_start(rows[4 * r:4 * r + 4, :], vec.rearrange("(t p) o -> t (p o)", p=P))
+        rows_t = bank(4, "rows_t", [P, P])
+        nc.tensor.transpose(rows_t[:], rows[:], ident[:])
+        cols = sb("cols", [P, 12], F32)
+        nc.scalar.activation(cols[:], rows_t[:, 0:12], ACT.Copy)
+        neg_th = sb("neg_th", [P, 4], F32)
+        nc.scalar.activation(neg_th[:], cols[:, 4:8], ACT.Copy, scale=-1.0)
+        bias = sb("bias", [P, 4], F32)
+        for t in range(4):
+            nc.scalar.activation(bias[:, t:t + 1], neg_th[:, t:t + 1], ACT.Copy, scale=cols[:, t:t + 1])
+
+        xg = [sb("xg%d" % g, [P, S], U32) for g in range(3)]
+        dg_a = sb("dg_a", [P, 3 * CHUNK], U32)
+        dg_b = relay.tile([P, 3 * CHUNK], U32, name="dg_b", offset=0, align_bytes=64)
+        dg = [[tile[:, g * CHUNK:(g + 1) * CHUNK] for g in range(3)] for tile in (dg_a, dg_b)]
+
+        def gather_x(half):
+            for g in range(3):
+                nc.vector.tensor_copy(
+                    xg[g][:, half * HALF:(half + 1) * HALF],
+                    xw_win[:].indirect(entries(x_lists[g], half * HALF, HALF)),
+                )
+
+        def gather_d(c):
+            for g in range(3):
+                nc.vector.tensor_copy(dg[c][g], dw_win[:].indirect(entries(d_lists[g], c * CHUNK, CHUNK)))
+
+        h = [sb("h_a", [P, 2, S], F32), sb("h_b", [P, 2, S], F32)]
+        sg = [sb("sg%d" % t, [P, S], F32) for t in range(4)]
+        z = [sb("z%d" % t, [P, S], BF16) for t in range(4)]
+
+        def h_rows(t):
+            return h[t // 2][:, t % 2, :]
+
+        def scatter_h(t, first, count):
+            nc.scalar.activation(
+                ds[t][:].indirect(entries(n1_sb, first, count)), h_rows(t)[:, first:first + count], ACT.Copy
+            )
+
+        def gate(t, first, count):
+            nc.scalar.activation(
+                sg[t][:, first:first + count], ds[t][:].indirect(entries(n2_sb, first, count)), ACT.Sigmoid,
+                bias=bias[:, t:t + 1], scale=cols[:, t:t + 1],
+            )
+
+        gather_x(0)
+        gather_d(0)
+        for half in range(2):
+            if half == 1:
+                gather_x(1)
+            acc = bank(half, "acc_a%d" % half, [P, 2, HALF])
+            for g in range(3):
+                for t in range(2):
+                    x0 = g * S + half * HALF
+                    d0 = 3 * S + g * CHUNK + t * P
+                    nc.tensor.matmul_mx(
+                        acc[:, t, :],
+                        lhsT=dg[0][g][:, t * P:(t + 1) * P].bitcast(FP8X4),
+                        lhsT_scale=plane_a[:, d0:d0 + P],
+                        rhs=xg[g][:, half * HALF:(half + 1) * HALF].bitcast(FP8X4),
+                        rhs_scale=plane_a[:, x0:x0 + HALF],
+                        start=(g == 0 and t == 0),
+                        stop=(g == 2 and t == 1),
+                    )
+            nc.scalar.activation(h[0][:, :, half * HALF:(half + 1) * HALF], acc[:], ACT.Copy, scale=0.0625)
+            for t in range(2):
+                scatter_h(t, half * HALF, HALF)
+                if half == 1:
+                    gate(t, 0, S)
+
+        picked_b = relay.tile([P, 3 * CHUNK], U8, name="picked_b", offset=3072)
+        for g in range(3):
+            nc.vector.tensor_copy(
+                picked_b[:, g * CHUNK:(g + 1) * CHUNK], ds_win[:].indirect(entries(d_lists[g], CHUNK, CHUNK))
+            )
+        place_rows(nc.sync, plane_b, picked_b)
+        gather_d(1)
+        acc_b = [bank(2 + t, "acc_b%d" % t, [P, S]) for t in range(2)]
+        for g in range(3):
+            for t in range(2):
+                d0 = g * CHUNK + t * P
+                nc.tensor.matmul_mx(
+                    acc_b[t][:],
+                    lhsT=dg[1][g][:, t * P:(t + 1) * P].bitcast(FP8X4),
+                    lhsT_scale=plane_b[:, d0:d0 + P],
+                    rhs=xg[g][:].bitcast(FP8X4),
+                    rhs_scale=plane_a[:, g * S:(g + 1) * S],
+                    start=(g == 0),
+                    stop=(g == 2),
+                )
+        for t in range(2):
+            nc.vector.tensor_scalar(h[1][:, t, :], acc_b[t][:], 0.0625, None, ALU.mult)
+
+        w2w = load_words(nc.sync, "w2w", w2_words, "ds_win")
+        w1w = load_words(nc.sync, "w1w", w1_words, "dw_win")
+        plane_w = relay.tile([P, 2 * N], U8, name="plane_w", offset=3072, align_bytes=64)
+        nc.gpsimd.memset(plane_w[:].bitcast(I32), 0)
+        for i, src in enumerate((w2_scales, w1_scales)):
+            for s in range(4):
+                nc.sync.dma_start(
+                    plane_w[:].bitcast(I32)[s:P:32, i * (N // 4):(i + 1) * (N // 4)], src[0].bitcast(I32)[s:16:4, :]
+                )
+
+        scatter_h(2, 0, S)
+        gate(2, 0, S)
+        scatter_h(3, 0, S)
+        gate(3, 0, HALF)
+        gate(3, HALF, HALF)
+
+        picked_two = relay.tile([P, S], U8, name="picked_two", offset=1024)
+        nc.vector.tensor_copy(picked_two[:], xs_win[:].indirect(two_sb[:]))
+        place_rows(nc.sync, plane_two, picked_two)
+        xg_two = relay.tile([P, S], U32, name="xg_two", offset=0, align_bytes=64)
+        nc.vector.tensor_copy(xg_two[:], xw_win[:].indirect(two_sb[:]))
+
+        acc2 = [bank((2, 3, 6, 7)[m], "acc2_%d" % m, [P, S]) for m in range(4)]
+        for m in range(4):
+            nc.tensor.matmul_mx(
+                acc2[m][:],
+                lhsT=w2w[:, m * P:(m + 1) * P].bitcast(FP8X4),
+                lhsT_scale=plane_w[:, m * P:(m + 1) * P],
+                rhs=xg_two[:].bitcast(FP8X4),
+                rhs_scale=plane_two[:],
+                start=True,
+                stop=False,
+            )
+
+        zt_ps = [bank(4 + half, "zt_ps%d" % half, [P, H], BF16) for half in range(2)]
+        zt = [sb("zt%d" % half, [P, 2, P, 2], BF16) for half in range(2)]
+
+        def make_z(t, first, count):
+            nc.vector.scalar_tensor_tensor(
+                z[t][:, first:first + count], h_rows(t)[:, first:first + count], cols[:, 8 + t:9 + t],
+                sg[t][:, first:first + count], ALU.mult, ALU.mult,
+            )
+
+        def turn(t, half):
+            nc.tensor.transpose(
+                zt_ps[half][:, t * P:(t + 1) * P], z[t][:, half * HALF:(half + 1) * HALF], ident_bf[:]
+            )
+
+        def pair_up(copy, half, t0, t1):
+            copy(
+                zt[half][:, :, 32 * t0:32 * t1, :],
+                zt_ps[half][:, t0 * P:t1 * P].rearrange("j (a u e) -> j u a e", u=2, e=2),
+            )
+
+        for t in range(3):
+            make_z(t, 0, S)
+            for half in range(2):
+                turn(t, half)
+        for half in range(2):
+            pair_up(nc.vector.tensor_copy, half, 0, 3)
+        copies = (nc.vector.tensor_copy, nc.scalar.copy)
+        zq = sb("zq", [P, S], U32)
+        zs = sb("zs", [P, S], U8)
+        for half in range(2):
+            make_z(3, half * HALF, HALF)
+            turn(3, half)
+            pair_up(copies[half], half, 3, 4)
+            back = bank(half, "back%d" % half, [P, 2, HALF])
+            words = zt[half][:].rearrange("j u a e -> j (u a e)").bitcast(F32)
+            for u in range(2):
+                nc.tensor.transpose(back[:, u, :], words[:, u * P:(u + 1) * P], ident[:])
+            grouped = sb("grouped%d" % half, [P, 4 * HALF], BF16)
+            copies[half](
+                grouped[:].bitcast(F32).rearrange("p (j u) -> p j u", u=2), back[:].rearrange("p u j -> p j u")
+            )
+            cols_j = slice(half * HALF, (half + 1) * HALF)
+            nc.vector.quantize_mx(zq[:, cols_j].bitcast(FP8X4), zs[:, cols_j], grouped[:])
+            for m in range(4):
+                nc.tensor.matmul_mx(
+                    acc2[m][:, cols_j],
+                    lhsT=w1w[:, m * P:(m + 1) * P].bitcast(FP8X4),
+                    lhsT_scale=plane_w[:, N + m * P:N + (m + 1) * P],
+                    rhs=zq[:, cols_j].bitcast(FP8X4),
+                    rhs_scale=zs[:, cols_j],
+                    start=False,
+                    stop=(half == 1),
+                )
+
+        for m in range(4):
+            (nc.scalar.copy if m == 0 else nc.vector.tensor_copy)(h2[m][:, 0:S], acc2[m][:])
+        for m in range(4):
+            pa = sb("pa%d" % m, [P, W], F32)
+            pb = sb("pb%d" % m, [P, W], F32)
+            rb = sb("rb%d" % m, [P, W], F32)
+            ub = sb("ub%d" % m, [P, S], F32)
+            far = sb("far%d" % m, [P, S], F32)
+            res = sb("res%d" % m, [P, S], F32)
+            nc.scalar.activation(pa[:], h2[m][:].indirect(n3_sb[:]), ACT.Copy)
+            nc.scalar.activation(pb[:], h2[m][:].indirect(n4_sb[:]), ACT.Copy)
+            nc.vector.tensor_tensor(rb[:], pa[:], pb[:], ALU.max)
+            nc.scalar.activation(ub[:].indirect(n5_sb[:]), pb[:], ACT.Copy)
+            nc.scalar.activation(far[:], h2[m][:].indirect(n7_sb[:]), ACT.Copy)
+            nc.scalar.activation(ub[:].indirect(n6_sb[:]), rb[:], ACT.Copy)
+            nc.vector.tensor_tensor(res[:], ub[:], far[:], ALU.subtract)
+            nc.sync.dma_start(out[m * P:(m + 1) * P, :], res[:])

@@ -62,19 +62,21 @@ def tile_picked_mthhznterlcpsw_none_p_kernel(
         def entries(tile, first, count):
             return tile[:, first // 16:(first + count) // 16]
 
-        def load_scale_window(name, src):
-            cols = src.shape[2]
-            tile = sb(name, [P, cols], U8)
-            nc.sync.dma_start(
-                tile[:].bitcast(I32), src[0].bitcast(I32).unsqueeze(1).to_broadcast([16, 8, cols // 4])
-            )
-            return tile
+        xs_win = sb("xs_win", [P, T], U8)
+        ds_win = sb("ds_win", [P, G], U8)
+        nc.gpsimd.memset(xs_win[:].bitcast(I32), 0)
+        nc.gpsimd.memset(ds_win[:].bitcast(I32), 0)
+        ident = sb("ident", [P, P], F32)
+        make_identity(nc, ident[:])
+        warm_in = sb("warm_in", [P, 1], F32)
+        warm_out = sb("warm_out", [P, 1], F32)
+        nc.vector.memset(warm_in[:], 0.0)
+        nc.scalar.activation(warm_out[:], warm_in[:], ACT.Sigmoid)
 
-        xs_win = load_scale_window("xs_win", x_scales)
+        nc.sync.dma_start(xs_win[:].bitcast(I32)[0:P:8, :], x_scales[0].bitcast(I32))
         x_lists = [load_list("offs_sb", offs), load_list("hz_sb", hz), load_list("hy_sb", hy)]
-        ds_win = load_scale_window("ds_win", d_scales)
+        nc.sync.dma_start(ds_win[:].bitcast(I32)[0:P:8, :], d_scales[0].bitcast(I32))
         d_lists = [load_list("k1_sb", k1), load_list("k2_sb", k2), load_list("k3_sb", k3)]
-        xw_win = load_words(nc.sync, "xw_win", x_words)
         dw_win = load_words(nc.sync, "dw_win", d_words)
         n1_sb = load_list("n1_sb", n1)
         n2_sb = load_list("n2_sb", n2)
@@ -82,22 +84,16 @@ def tile_picked_mthhznterlcpsw_none_p_kernel(
         n3_sb = load_list("n3_sb", n3)
         n4_sb = load_list("n4_sb", n4)
         n5_sb = load_list("n5_sb", n5)
-        n7_sb = load_list("n7_sb", n7)
-        n6_sb = load_list("n6_sb", n6)
+        xw_win = load_words(nc.sync, "xw_win", x_words)
         plane_a = zeroed_plane("plane_a", 3 * S + 3 * CHUNK)
         plane_b = zeroed_plane("plane_b", 3 * CHUNK)
-        plane_two = zeroed_plane("plane_two", S)
 
-        ident = sb("ident", [P, P], F32)
-        make_identity(nc, ident[:])
         ds = [sb("ds%d" % t, [P, DS_COLS], F32) for t in range(4)]
         h2 = [sb("h2_%d" % m, [P, H2_COLS], F32) for m in range(4)]
         for t in range(4):
-            nc.gpsimd.memset(ds[t][:, S:], 0.0)
+            nc.vector.memset(ds[t][:, S:], 0.0)
         for m in range(4):
             nc.gpsimd.memset(h2[m][:, S:], 0.0)
-        ident_bf = sb("ident_bf", [P, P], BF16)
-        nc.scalar.activation(ident_bf[:], ident[:], ACT.Copy)
 
         picked_a = relay.tile([P, 3 * S + 3 * CHUNK], U8, name="picked_a", offset=3008)
         for g in range(3):
@@ -107,21 +103,21 @@ def tile_picked_mthhznterlcpsw_none_p_kernel(
                 picked_a[:, 3 * S + g * CHUNK:3 * S + (g + 1) * CHUNK],
                 ds_win[:].indirect(entries(d_lists[g], 0, CHUNK)),
             )
-        place_rows(nc.scalar, plane_a, picked_a)
+        place_rows(nc.sync, plane_a, picked_a)
+        n7_sb = load_list("n7_sb", n7)
+        n6_sb = load_list("n6_sb", n6)
 
-        rows = relay.tile([P, P], F32, name="rows", offset=3840)
-        nc.gpsimd.memset(rows[:], 0.0)
-        for r, vec in enumerate((sl, th, gn)):
-            nc.sync.dma_start(rows[4 * r:4 * r + 4, :], vec.rearrange("(t p) o -> t (p o)", p=P))
-        rows_t = bank(4, "rows_t", [P, P])
-        nc.tensor.transpose(rows_t[:], rows[:], ident[:])
-        cols = sb("cols", [P, 12], F32)
-        nc.scalar.activation(cols[:], rows_t[:, 0:12], ACT.Copy)
-        neg_th = sb("neg_th", [P, 4], F32)
-        nc.scalar.activation(neg_th[:], cols[:, 4:8], ACT.Copy, scale=-1.0)
+        def load_rows(name, vec, offset):
+            tile = relay.tile([P, 4], F32, name=name, offset=offset, align_bytes=64)
+            with nc.allow_non_contiguous_dma(reason="one value a partition and row tile"):
+                nc.sync.dma_start(tile[:], vec.rearrange("(t p) o -> p (t o)", p=P))
+            return tile
+
+        sl_sb = load_rows("sl_sb", sl, 4096)
+        th_sb = load_rows("th_sb", th, 4160)
+        gn_sb = load_rows("gn_sb", gn, 4224)
         bias = sb("bias", [P, 4], F32)
-        for t in range(4):
-            nc.scalar.activation(bias[:, t:t + 1], neg_th[:, t:t + 1], ACT.Copy, scale=cols[:, t:t + 1])
+        nc.vector.scalar_tensor_tensor(bias[:], th_sb[:], -1.0, sl_sb[:], ALU.mult, ALU.mult)
 
         xg = [sb("xg%d" % g, [P, S], U32) for g in range(3)]
         dg_a = sb("dg_a", [P, 3 * CHUNK], U32)
@@ -141,7 +137,6 @@ def tile_picked_mthhznterlcpsw_none_p_kernel(
 
         h = [sb("h_a", [P, 2, S], F32), sb("h_b", [P, 2, S], F32)]
         sg = [sb("sg%d" % t, [P, S], F32) for t in range(4)]
-        z = [sb("z%d" % t, [P, S], BF16) for t in range(4)]
 
         def h_rows(t):
             return h[t // 2][:, t % 2, :]
@@ -154,11 +149,11 @@ def tile_picked_mthhznterlcpsw_none_p_kernel(
         def gate(t, first, count):
             nc.scalar.activation(
                 sg[t][:, first:first + count], ds[t][:].indirect(entries(n2_sb, first, count)), ACT.Sigmoid,
-                bias=bias[:, t:t + 1], scale=cols[:, t:t + 1],
+                bias=bias[:, t:t + 1], scale=sl_sb[:, t:t + 1],
             )
 
-        gather_x(0)
         gather_d(0)
+        gather_x(0)
         for half in range(2):
             if half == 1:
                 gather_x(1)
@@ -189,9 +184,15 @@ def tile_picked_mthhznterlcpsw_none_p_kernel(
             )
         place_rows(nc.sync, plane_b, picked_b)
         gather_d(1)
+        for s in range(4):
+            nc.sync.dma_start(xs_win[:].bitcast(I32)[4 + s:P:32, :], x_scales[0].bitcast(I32)[s:16:4, :])
+        picked_two = relay.tile([P, S], U8, name="picked_two", offset=3840, align_bytes=64)
+        nc.vector.tensor_copy(picked_two[:], xs_win[:].indirect(two_sb[:]))
+        xg_two = relay.tile([P, S], U32, name="xg_two", offset=4480, align_bytes=64)
+        nc.vector.tensor_copy(xg_two[:], xw_win[:].indirect(two_sb[:]))
         acc_b = [bank(2 + t, "acc_b%d" % t, [P, S]) for t in range(2)]
-        for g in range(3):
-            for t in range(2):
+        for t in range(2):
+            for g in range(3):
                 d0 = g * CHUNK + t * P
                 nc.tensor.matmul_mx(
                     acc_b[t][:],
@@ -207,71 +208,64 @@ def tile_picked_mthhznterlcpsw_none_p_kernel(
 
         w2w = load_words(nc.sync, "w2w", w2_words, "ds_win")
         w1w = load_words(nc.sync, "w1w", w1_words, "dw_win")
-        plane_w = relay.tile([P, 2 * N], U8, name="plane_w", offset=3072, align_bytes=64)
-        nc.gpsimd.memset(plane_w[:].bitcast(I32), 0)
+        plane_w = plane_a[:, 3 * S:3 * S + N]
         for i, src in enumerate((w2_scales, w1_scales)):
             for s in range(4):
                 nc.sync.dma_start(
-                    plane_w[:].bitcast(I32)[s:P:32, i * (N // 4):(i + 1) * (N // 4)], src[0].bitcast(I32)[s:16:4, :]
+                    plane_w.bitcast(I32)[4 * (i + 1) + s:P:32, :], src[0].bitcast(I32)[s:16:4, :]
                 )
 
         scatter_h(2, 0, S)
-        gate(2, 0, S)
         scatter_h(3, 0, S)
-        gate(3, 0, HALF)
-        gate(3, HALF, HALF)
+        for half in range(2):
+            for t in (2, 3):
+                gate(t, half * HALF, HALF)
 
-        picked_two = relay.tile([P, S], U8, name="picked_two", offset=1024)
-        nc.vector.tensor_copy(picked_two[:], xs_win[:].indirect(two_sb[:]))
-        place_rows(nc.sync, plane_two, picked_two)
-        xg_two = relay.tile([P, S], U32, name="xg_two", offset=0, align_bytes=64)
-        nc.vector.tensor_copy(xg_two[:], xw_win[:].indirect(two_sb[:]))
-
-        acc2 = [bank((2, 3, 6, 7)[m], "acc2_%d" % m, [P, S]) for m in range(4)]
+        acc2 = [bank(4 + m, "acc2_%d" % m, [P, S]) for m in range(4)]
         for m in range(4):
             nc.tensor.matmul_mx(
                 acc2[m][:],
                 lhsT=w2w[:, m * P:(m + 1) * P].bitcast(FP8X4),
-                lhsT_scale=plane_w[:, m * P:(m + 1) * P],
+                lhsT_scale=plane_w[4:P, m * P:(m + 1) * P],
                 rhs=xg_two[:].bitcast(FP8X4),
-                rhs_scale=plane_two[:],
+                rhs_scale=picked_two[4:P, :],
                 start=True,
                 stop=False,
             )
 
-        zt_ps = [bank(4 + half, "zt_ps%d" % half, [P, H], BF16) for half in range(2)]
         zt = [sb("zt%d" % half, [P, 2, P, 2], BF16) for half in range(2)]
+        turn_bank = (2, 0)
+        hgt = [sb("hgt%d" % c, [P, 2, 2, 64, 2], F32) for c in range(2)]
 
-        def make_z(t, first, count):
-            nc.vector.scalar_tensor_tensor(
-                z[t][:, first:first + count], h_rows(t)[:, first:first + count], cols[:, 8 + t:9 + t],
-                sg[t][:, first:first + count], ALU.mult, ALU.mult,
+        def turned(name, c, half, sources):
+            tile = bank(turn_bank[c] + half, "%s%d_%d" % (name, c, half), [P, 2 * P])
+            for t in range(2):
+                nc.tensor.transpose(
+                    tile[:, t * P:(t + 1) * P], sources[t][:, half * HALF:(half + 1) * HALF], ident[:]
+                )
+            return tile[:].rearrange("j (a u e) -> j u a e", u=2, e=2)
+
+        def make_zt(c, half):
+            nc.vector.tensor_tensor(
+                zt[half][:, :, 64 * c:64 * (c + 1), :],
+                turned("sgt", c, half, [sg[2 * c][:], sg[2 * c + 1][:]]),
+                hgt[c][:, half],
+                ALU.mult,
             )
 
-        def turn(t, half):
-            nc.tensor.transpose(
-                zt_ps[half][:, t * P:(t + 1) * P], z[t][:, half * HALF:(half + 1) * HALF], ident_bf[:]
-            )
-
-        def pair_up(copy, half, t0, t1):
-            copy(
-                zt[half][:, :, 32 * t0:32 * t1, :],
-                zt_ps[half][:, t0 * P:t1 * P].rearrange("j (a u e) -> j u a e", u=2, e=2),
-            )
-
-        for t in range(3):
-            make_z(t, 0, S)
+        for c in range(2):
+            hg = sb("hg%d" % c, [P, 2, S], F32)
+            for t in range(2):
+                nc.vector.tensor_scalar(hg[:, t, :], h[c][:, t, :], gn_sb[:, 2 * c + t:2 * c + t + 1], None, ALU.mult)
             for half in range(2):
-                turn(t, half)
+                nc.vector.tensor_copy(hgt[c][:, half], turned("hgt", c, half, [hg[:, 0, :], hg[:, 1, :]]))
         for half in range(2):
-            pair_up(nc.vector.tensor_copy, half, 0, 3)
+            make_zt(0, half)
         copies = (nc.vector.tensor_copy, nc.scalar.copy)
         zq = sb("zq", [P, S], U32)
         zs = sb("zs", [P, S], U8)
         for half in range(2):
-            make_z(3, half * HALF, HALF)
-            turn(3, half)
-            pair_up(copies[half], half, 3, 4)
+            make_zt(1, half)
             back = bank(half, "back%d" % half, [P, 2, HALF])
             words = zt[half][:].rearrange("j u a e -> j (u a e)").bitcast(F32)
             for u in range(2):
@@ -286,7 +280,7 @@ def tile_picked_mthhznterlcpsw_none_p_kernel(
                 nc.tensor.matmul_mx(
                     acc2[m][:, cols_j],
                     lhsT=w1w[:, m * P:(m + 1) * P].bitcast(FP8X4),
-                    lhsT_scale=plane_w[:, N + m * P:N + (m + 1) * P],
+                    lhsT_scale=plane_w[8:P, m * P:(m + 1) * P],
                     rhs=zq[:, cols_j].bitcast(FP8X4),
                     rhs_scale=zs[:, cols_j],
                     start=False,
@@ -308,5 +302,8 @@ def tile_picked_mthhznterlcpsw_none_p_kernel(
             nc.scalar.activation(ub[:].indirect(n5_sb[:]), pb[:], ACT.Copy)
             nc.scalar.activation(far[:], h2[m][:].indirect(n7_sb[:]), ACT.Copy)
             nc.scalar.activation(ub[:].indirect(n6_sb[:]), rb[:], ACT.Copy)
-            nc.vector.tensor_tensor(res[:], ub[:], far[:], ALU.subtract)
-            nc.sync.dma_start(out[m * P:(m + 1) * P, :], res[:])
+            pieces = 2 if m == 3 else 1
+            for i in range(pieces):
+                part = slice(i * S // pieces, (i + 1) * S // pieces)
+                nc.vector.tensor_tensor(res[:, part], ub[:, part], far[:, part], ALU.subtract)
+                (nc.sync, nc.scalar)[i].dma_start(out[m * P:(m + 1) * P, part], res[:, part])

from contextlib import ExitStack

import concourse.mybir as mybir
from concourse.masks import make_identity

FLOPS = 671088640

F32 = mybir.dt.float32
BF16 = mybir.dt.bfloat16
I32 = mybir.dt.int32
U32 = mybir.dt.uint32
U16 = mybir.dt.uint16
U8 = mybir.dt.uint8
FP8X4 = mybir.dt.float8_e4m3fn_x4
ACT = mybir.ActivationFunctionType
ALU = mybir.AluOpType

P = 128
T, G, S, H, N, W = 1024, 2048, 256, 512, 512, 128
HALF = S // 2
CHUNK = 256
DS_COLS = 2 * S
H2_COLS = S + 16


def tile_picked_mthhznterlcpsw_none_p_kernel(
    tc, x_words, x_scales, d_words, d_scales, sl, th, gn, w1_words, w1_scales, w2_words, w2_scales,
    offs, k1, hz, k2, hy, k3, n1, n2, two, n3, n4, n5, n6, n7, out,
):
    nc = tc.nc
    with ExitStack() as ctx:
        lists = ctx.enter_context(tc.tile_pool(name="lists", bufs=1))
        keep = ctx.enter_context(tc.tile_pool(name="keep", bufs=1))
        relay = ctx.enter_context(tc.tile_pool(name="relay", bufs=1))
        psum = ctx.enter_context(tc.psum_pool(name="psum", bufs=1))

        def sb(name, shape, dtype, tag=None):
            return keep.tile(shape, dtype, name=name, tag=tag or name, align_bytes=64)

        def bank(index, name, shape, dtype=F32):
            return psum.tile(shape, dtype, name=name, tag="bank%d" % index)

        def load_list(name, src):
            tile = lists.tile(list(src.shape), U16, name=name)
            nc.sync.dma_start(tile[:], src)
            return tile

        def zeroed_plane(name, cols, tag=None):
            plane = sb(name, [P, cols], U8, tag)
            nc.vector.memset(plane[:].bitcast(I32), 0)
            return plane

        def load_words(queue, name, src, tag=None):
            tile = sb(name, [P, src.shape[2]], U32, tag)
            queue.dma_start(tile[:].bitcast(I32), src[0].rearrange("p n t -> p (n t)").bitcast(I32))
            return tile

        def place_rows(queue, plane, picked):
            for s in range(4):
                queue.dma_start(plane[:].bitcast(I32)[s:P:32, :], picked[:].bitcast(I32)[8 * s:P:32, :])

        def entries(tile, first, count):
            return tile[:, first // 16:(first + count) // 16]

        xs_win = sb("xs_win", [P, T], U8)
        ds_win = sb("ds_win", [P, G], U8)
        nc.gpsimd.memset(xs_win[:].bitcast(I32), 0)
        nc.gpsimd.memset(ds_win[:].bitcast(I32), 0)
        ident = sb("ident", [P, P], F32)
        make_identity(nc, ident[:])
        warm_in = sb("warm_in", [P, 1], F32)
        warm_out = sb("warm_out", [P, 1], F32)
        nc.vector.memset(warm_in[:], 0.0)
        nc.scalar.activation(warm_out[:], warm_in[:], ACT.Sigmoid)

        nc.sync.dma_start(xs_win[:].bitcast(I32)[0:P:8, :], x_scales[0].bitcast(I32))
        x_lists = [load_list("offs_sb", offs), load_list("hz_sb", hz), load_list("hy_sb", hy)]
        nc.sync.dma_start(ds_win[:].bitcast(I32)[0:P:8, :], d_scales[0].bitcast(I32))
        d_lists = [load_list("k1_sb", k1), load_list("k2_sb", k2), load_list("k3_sb", k3)]
        dw_win = load_words(nc.sync, "dw_win", d_words)
        n1_sb = load_list("n1_sb", n1)
        n2_sb = load_list("n2_sb", n2)
        two_sb = load_list("two_sb", two)
        n3_sb = load_list("n3_sb", n3)
        n4_sb = load_list("n4_sb", n4)
        n5_sb = load_list("n5_sb", n5)
        xw_win = load_words(nc.sync, "xw_win", x_words)
        plane_a = zeroed_plane("plane_a", 3 * S + 3 * CHUNK)
        plane_b = zeroed_plane("plane_b", 3 * CHUNK)

        ds = [sb("ds%d" % t, [P, DS_COLS], F32) for t in range(4)]
        h2 = [sb("h2_%d" % m, [P, H2_COLS], F32) for m in range(4)]
        for t in range(4):
            nc.vector.memset(ds[t][:, S:], 0.0)
        for m in range(4):
            nc.gpsimd.memset(h2[m][:, S:], 0.0)

        picked_a = relay.tile([P, 3 * S + 3 * CHUNK], U8, name="picked_a", offset=3008)
        for g in range(3):
            nc.vector.tensor_copy(picked_a[:, g * S:(g + 1) * S], xs_win[:].indirect(x_lists[g][:]))
        for g in range(3):
            nc.vector.tensor_copy(
                picked_a[:, 3 * S + g * CHUNK:3 * S + (g + 1) * CHUNK],
                ds_win[:].indirect(entries(d_lists[g], 0, CHUNK)),
            )
        place_rows(nc.sync, plane_a, picked_a)
        n7_sb = load_list("n7_sb", n7)
        n6_sb = load_list("n6_sb", n6)

        def load_rows(name, vec, offset):
            tile = relay.tile([P, 4], F32, name=name, offset=offset, align_bytes=64)
            with nc.allow_non_contiguous_dma(reason="one value a partition and row tile"):
                nc.sync.dma_start(tile[:], vec.rearrange("(t p) o -> p (t o)", p=P))
            return tile

        sl_sb = load_rows("sl_sb", sl, 4096)
        th_sb = load_rows("th_sb", th, 4160)
        gn_sb = load_rows("gn_sb", gn, 4224)
        bias = sb("bias", [P, 4], F32)
        nc.vector.scalar_tensor_tensor(bias[:], th_sb[:], -1.0, sl_sb[:], ALU.mult, ALU.mult)

        xg = [sb("xg%d" % g, [P, S], U32) for g in range(3)]
        dg_a = sb("dg_a", [P, 3 * CHUNK], U32)
        dg_b = relay.tile([P, 3 * CHUNK], U32, name="dg_b", offset=0, align_bytes=64)
        dg = [[tile[:, g * CHUNK:(g + 1) * CHUNK] for g in range(3)] for tile in (dg_a, dg_b)]

        def gather_x(half):
            for g in range(3):
                nc.vector.tensor_copy(
                    xg[g][:, half * HALF:(half + 1) * HALF],
                    xw_win[:].indirect(entries(x_lists[g], half * HALF, HALF)),
                )

        def gather_d(c):
            for g in range(3):
                nc.vector.tensor_copy(dg[c][g], dw_win[:].indirect(entries(d_lists[g], c * CHUNK, CHUNK)))

        h = [sb("h_a", [P, 2, S], F32), sb("h_b", [P, 2, S], F32)]
        sg = [sb("sg%d" % t, [P, S], F32) for t in range(4)]

        def h_rows(t):
            return h[t // 2][:, t % 2, :]

        def scatter_h(t, first, count):
            nc.scalar.activation(
                ds[t][:].indirect(entries(n1_sb, first, count)), h_rows(t)[:, first:first + count], ACT.Copy
            )

        def gate(t, first, count):
            nc.scalar.activation(
                sg[t][:, first:first + count], ds[t][:].indirect(entries(n2_sb, first, count)), ACT.Sigmoid,
                bias=bias[:, t:t + 1], scale=sl_sb[:, t:t + 1],
            )

        gather_d(0)
        gather_x(0)
        for half in range(2):
            if half == 1:
                gather_x(1)
            acc = bank(half, "acc_a%d" % half, [P, 2, HALF])
            for g in range(3):
                for t in range(2):
                    x0 = g * S + half * HALF
                    d0 = 3 * S + g * CHUNK + t * P
                    nc.tensor.matmul_mx(
                        acc[:, t, :],
                        lhsT=dg[0][g][:, t * P:(t + 1) * P].bitcast(FP8X4),
                        lhsT_scale=plane_a[:, d0:d0 + P],
                        rhs=xg[g][:, half * HALF:(half + 1) * HALF].bitcast(FP8X4),
                        rhs_scale=plane_a[:, x0:x0 + HALF],
                        start=(g == 0 and t == 0),
                        stop=(g == 2 and t == 1),
                    )
            nc.scalar.activation(h[0][:, :, half * HALF:(half + 1) * HALF], acc[:], ACT.Copy, scale=0.0625)
            for t in range(2):
                scatter_h(t, half * HALF, HALF)
                if half == 1:
                    gate(t, 0, S)

        picked_b = relay.tile([P, 3 * CHUNK], U8, name="picked_b", offset=3072)
        for g in range(3):
            nc.vector.tensor_copy(
                picked_b[:, g * CHUNK:(g + 1) * CHUNK], ds_win[:].indirect(entries(d_lists[g], CHUNK, CHUNK))
            )
        place_rows(nc.sync, plane_b, picked_b)
        gather_d(1)
        for s in range(4):
            nc.sync.dma_start(xs_win[:].bitcast(I32)[4 + s:P:32, :], x_scales[0].bitcast(I32)[s:16:4, :])
        picked_two = relay.tile([P, S], U8, name="picked_two", offset=3840, align_bytes=64)
        nc.vector.tensor_copy(picked_two[:], xs_win[:].indirect(two_sb[:]))
        xg_two = relay.tile([P, S], U32, name="xg_two", offset=4480, align_bytes=64)
        nc.vector.tensor_copy(xg_two[:], xw_win[:].indirect(two_sb[:]))
        acc_b = [bank(2 + t, "acc_b%d" % t, [P, S]) for t in range(2)]
        for t in range(2):
            for g in range(3):
                d0 = g * CHUNK + t * P
                nc.tensor.matmul_mx(
                    acc_b[t][:],
                    lhsT=dg[1][g][:, t * P:(t + 1) * P].bitcast(FP8X4),
                    lhsT_scale=plane_b[:, d0:d0 + P],
                    rhs=xg[g][:].bitcast(FP8X4),
                    rhs_scale=plane_a[:, g * S:(g + 1) * S],
                    start=(g == 0),
                    stop=(g == 2),
                )
        for t in range(2):
            nc.vector.tensor_scalar(h[1][:, t, :], acc_b[t][:], 0.0625, None, ALU.mult)

        w2w = load_words(nc.sync, "w2w", w2_words, "ds_win")
        w1w = load_words(nc.sync, "w1w", w1_words, "dw_win")
        plane_w = plane_a[:, 3 * S:3 * S + N]
        for i, src in enumerate((w2_scales, w1_scales)):
            for s in range(4):
                nc.sync.dma_start(
                    plane_w.bitcast(I32)[4 * (i + 1) + s:P:32, :], src[0].bitcast(I32)[s:16:4, :]
                )

        scatter_h(2, 0, S)
        scatter_h(3, 0, S)
        for half in range(2):
            for t in (2, 3):
                gate(t, half * HALF, HALF)

        acc2 = [bank(4 + m, "acc2_%d" % m, [P, S]) for m in range(4)]
        for m in range(4):
            nc.tensor.matmul_mx(
                acc2[m][:],
                lhsT=w2w[:, m * P:(m + 1) * P].bitcast(FP8X4),
                lhsT_scale=plane_w[4:P, m * P:(m + 1) * P],
                rhs=xg_two[:].bitcast(FP8X4),
                rhs_scale=picked_two[4:P, :],
                start=True,
                stop=False,
            )

        zt = [sb("zt%d" % half, [P, 2, P, 2], BF16) for half in range(2)]
        turn_bank = (2, 0)
        hgt = [sb("hgt%d" % c, [P, 2, 2, 64, 2], F32) for c in range(2)]

        def turned(name, c, half, sources):
            tile = bank(turn_bank[c] + half, "%s%d_%d" % (name, c, half), [P, 2 * P])
            for t in range(2):
                nc.tensor.transpose(
                    tile[:, t * P:(t + 1) * P], sources[t][:, half * HALF:(half + 1) * HALF], ident[:]
                )
            return tile[:].rearrange("j (a u e) -> j u a e", u=2, e=2)

        def make_zt(c, half):
            nc.vector.tensor_tensor(
                zt[half][:, :, 64 * c:64 * (c + 1), :],
                turned("sgt", c, half, [sg[2 * c][:], sg[2 * c + 1][:]]),
                hgt[c][:, half],
                ALU.mult,
            )

        for c in range(2):
            hg = sb("hg%d" % c, [P, 2, S], F32)
            for t in range(2):
                nc.vector.tensor_scalar(hg[:, t, :], h[c][:, t, :], gn_sb[:, 2 * c + t:2 * c + t + 1], None, ALU.mult)
            for half in range(2):
                nc.vector.tensor_copy(hgt[c][:, half], turned("hgt", c, half, [hg[:, 0, :], hg[:, 1, :]]))
        for half in range(2):
            make_zt(0, half)
        copies = (nc.vector.tensor_copy, nc.scalar.copy)
        zq = sb("zq", [P, S], U32)
        zs = sb("zs", [P, S], U8)
        for half in range(2):
            make_zt(1, half)
            back = bank(half, "back%d" % half, [P, 2, HALF])
            words = zt[half][:].rearrange("j u a e -> j (u a e)").bitcast(F32)
            for u in range(2):
                nc.tensor.transpose(back[:, u, :], words[:, u * P:(u + 1) * P], ident[:])
            grouped = sb("grouped%d" % half, [P, 4 * HALF], BF16)
            copies[half](
                grouped[:].bitcast(F32).rearrange("p (j u) -> p j u", u=2), back[:].rearrange("p u j -> p j u")
            )
            cols_j = slice(half * HALF, (half + 1) * HALF)
            nc.vector.quantize_mx(zq[:, cols_j].bitcast(FP8X4), zs[:, cols_j], grouped[:])
            for m in range(4):
                nc.tensor.matmul_mx(
                    acc2[m][:, cols_j],
                    lhsT=w1w[:, m * P:(m + 1) * P].bitcast(FP8X4),
                    lhsT_scale=plane_w[8:P, m * P:(m + 1) * P],
                    rhs=zq[:, cols_j].bitcast(FP8X4),
                    rhs_scale=zs[:, cols_j],
                    start=False,
                    stop=(half == 1),
                )

        for m in range(4):
            (nc.scalar.copy if m == 0 else nc.vector.tensor_copy)(h2[m][:, 0:S], acc2[m][:])
        for m in range(4):
            pa = sb("pa%d" % m, [P, W], F32)
            pb = sb("pb%d" % m, [P, W], F32)
            rb = sb("rb%d" % m, [P, W], F32)
            ub = sb("ub%d" % m, [P, S], F32)
            far = sb("far%d" % m, [P, S], F32)
            res = sb("res%d" % m, [P, S], F32)
            nc.scalar.activation(pa[:], h2[m][:].indirect(n3_sb[:]), ACT.Copy)
            nc.scalar.activation(pb[:], h2[m][:].indirect(n4_sb[:]), ACT.Copy)
            nc.vector.tensor_tensor(rb[:], pa[:], pb[:], ALU.max)
            nc.scalar.activation(ub[:].indirect(n5_sb[:]), pb[:], ACT.Copy)
            nc.scalar.activation(far[:], h2[m][:].indirect(n7_sb[:]), ACT.Copy)
            nc.scalar.activation(ub[:].indirect(n6_sb[:]), rb[:], ACT.Copy)
            pieces = 2 if m == 3 else 1
            for i in range(pieces):
                part = slice(i * S // pieces, (i + 1) * S // pieces)
                nc.vector.tensor_tensor(res[:, part], ub[:, part], far[:, part], ALU.subtract)
                (nc.sync, nc.scalar)[i].dma_start(out[m * P:(m + 1) * P, part], res[:, part])
